import numpy as np
import ml_dtypes


def mxq(x, axis, fmt="e4m3"):
    dtype, down = {"e4m3": (ml_dtypes.float8_e4m3fn, 7), "e5m2": (ml_dtypes.float8_e5m2, 14)}[fmt]
    v = np.moveaxis(np.asarray(x, np.float32).astype(ml_dtypes.bfloat16).astype(np.float64), axis, -1)
    blocks = v.reshape(v.shape[:-1] + (-1, 32))
    amax = np.abs(blocks).max(-1, keepdims=True)
    byte = np.maximum(np.where(amax > 0, np.frexp(amax)[1] - 1 + 127, 0) - down, 1)
    scale = np.exp2(byte - 127.0)
    codes = (blocks / scale).astype(np.float32).astype(dtype).astype(np.float64)
    return np.moveaxis((codes * scale).reshape(v.shape), -1, axis)


WIDE = False


def mx_kscale(k):
    if not WIDE:
        return np.ones(k)
    levels = np.array([10, -10, 5, -5, 0])
    if k % 512:
        return np.exp2(np.random.permutation(np.resize(levels, k // 32))).repeat(32)
    a = np.empty((k // 512, 16))
    for p in range(k // 512):
        a[p, :8] = np.random.permutation(np.resize(levels, 8))
        for g in range(8):
            far = levels[np.abs(levels - a[p, g]) >= 10]
            a[p, g + 8] = far[np.random.randint(len(far))]
    return np.exp2(a.ravel()).repeat(32)


def f64(x):
    return np.asarray(x).astype(np.float64)


def striped(idx):
    return np.tile(idx.reshape(-1, 16).T, (8, 1)).astype(np.uint16)


def unstriped(offs):
    return offs[:16].T.reshape(-1).astype(np.int64)


def gelu(v):
    return 0.5 * v * (1.0 + np.tanh(np.sqrt(2.0 / np.pi) * (v + 0.044715 * v**3)))


K, T, E, C, H, N = 512, 512, 8, 128, 1024, 256


def by_expert(wq, xq):
    return np.concatenate([wq[e].T @ xq[:, e * C:(e + 1) * C] for e in range(E)], axis=1)


def setup_inputs():
    n = np.random.standard_normal
    s = mx_kscale(K)[:, None]
    u = mx_kscale(H)
    first = np.random.permutation(np.repeat(np.arange(E), T // E))
    second = (first + 1 + np.random.permutation(np.repeat(np.arange(E - 1), -(-T // (E - 1)))[:T])) % E
    while np.bincount(second, minlength=E).max() != T // E:
        load = np.bincount(second, minlength=E); hi, lo = int(load.argmax()), int(load.argmin())
        t = np.flatnonzero((second == hi) & (first != lo))[0]; second[t] = lo
    slot_token = np.empty(E * C, np.int64); pos = np.empty((2, T), np.int64); fill = np.zeros(E, np.int64)
    place = np.stack([np.random.permutation(C) for _ in range(E)])
    for r, deal in enumerate((first, second)):
        for t in np.random.permutation(T):
            e = deal[t]; j = e * C + place[e, fill[e]]; fill[e] += 1; slot_token[j] = t; pos[r, t] = j
    g = np.random.uniform(0.2, 0.8, T)
    return {
        "xT": (n((K, T)) * s).astype(np.float32),
        "w1": (n((E, K, H)) / np.sqrt(K) / s[None] * u[None, None, :]).astype(np.float32),
        "w2": (n((E, H, N)) / np.sqrt(H) / u[None, :, None]).astype(np.float32),
        "gate": np.stack([np.tile(g, (N, 1)), np.tile(1.0 - g, (N, 1))]).astype(np.float32),
        "offs": striped(slot_token),
        "pos1": striped(pos[0]),
        "pos2": striped(pos[1]),
    }


def reference(xT, w1, w2, gate, offs, pos1, pos2):
    idx = unstriped(offs)
    xq = mxq(f64(xT)[:, idx], 0, "e4m3")
    h = gelu(by_expert(mxq(f64(w1), 1, "e4m3"), xq))
    y = by_expert(mxq(f64(w2), 1, "e4m3"), mxq(h, 0, "e4m3"))
    return f64(gate[0]) * y[:, unstriped(pos1)] + f64(gate[1]) * y[:, unstriped(pos2)]

@@ -1,0 +1,251 @@
+from contextlib import ExitStack
+
+import concourse.mybir as mybir
+
+K, T, E, C, H, N = 512, 512, 8, 128, 1024, 256
+FLOPS = 2 * E * C * (K * H + H * N)
+
+F32 = mybir.dt.float32
+BF16 = mybir.dt.bfloat16
+U32 = mybir.dt.uint32
+U16 = mybir.dt.uint16
+U8 = mybir.dt.uint8
+FP8X4 = mybir.dt.float8_e4m3fn_x4
+GELU = mybir.ActivationFunctionType.Gelu_apprx_tanh
+MULT = mybir.AluOpType.mult
+ADD = mybir.AluOpType.add
+
+P = 128
+PACK = 4
+KP = P * PACK
+HG = H // KP
+NB = N // P
+GSL = 256
+NQ = E * HG
+M_VEC = 16
+C_VEC_LAST = 42
+LOADS1 = ((0,), (1,), (2, 3), (4, 5), (6,), (7,))
+FILL = 2
+QH = NQ // 2
+
+
+def copy_on(nc, scalar, dst, src):
+    if scalar:
+        nc.scalar.copy(out=dst, in_=src)
+    else:
+        nc.vector.tensor_copy(out=dst, in_=src)
+
+
+def spread_w1(nc, grp, raw, g, m0, m1, scalar):
+    src = raw[:, :, g * KP : (g + 1) * KP].rearrange("p j (m t) -> p m j t", t=PACK)
+    dst = grp.rearrange("p (t m j) -> p m j t", t=PACK, j=PACK)
+    copy_on(nc, scalar, dst[:, m0:m1], src[:, m0:m1])
+
+
+def spread_plain(nc, grp, raw, c0, c1, scalar):
+    src = raw.rearrange("p j (c i) -> p c j i", i=PACK)
+    dst = grp.rearrange("p (c i j) -> p c j i", i=PACK, j=PACK)
+    copy_on(nc, scalar, dst[:, c0:c1], src[:, c0:c1])
+
+
+def tile_routed_moe_kernel(tc, xT, w1, w2, gate, offs, pos1, pos2, out):
+    nc = tc.nc
+    with ExitStack() as ctx:
+        keep = ctx.enter_context(tc.tile_pool(name="keep", bufs=1))
+        rawp = ctx.enter_context(tc.tile_pool(name="rawp", bufs=3))
+        grpp = ctx.enter_context(tc.tile_pool(name="grpp", bufs=4))
+        codep = ctx.enter_context(tc.tile_pool(name="codep", bufs=6))
+        finp = ctx.enter_context(tc.tile_pool(name="finp", bufs=2))
+        psum = ctx.enter_context(tc.psum_pool(name="psum", bufs=2))
+
+        offs_t = keep.tile([P, E * C // 16], U16, name="offs_t")
+        nc.sync.dma_start(offs_t[:], offs)
+        xraw = rawp.tile([P, PACK, T], F32, name="xraw", tag="raw")
+        nc.sync.dma_start(out=xraw[:], in_=xT.rearrange("(p j) t -> p j t", j=PACK))
+
+        raw1 = {}
+        raw2 = {}
+        stage2 = {}
+        grp1 = {}
+        c1 = {}
+        s1 = {}
+        c2 = {}
+        s2 = {}
+        ps1 = {}
+        ps2 = {}
+        hg = {}
+        hc = {}
+        hs = {}
+
+        def load_w1(es):
+            t1 = rawp.tile([P, len(es), PACK, H], F32, name="raw1", tag="raw")
+            nc.sync.dma_start(
+                out=t1[:], in_=w1[es[0] : es[0] + len(es)].rearrange("e (p j) h -> p e j h", j=PACK)
+            )
+            for k, e in enumerate(es):
+                raw1[e] = t1[:, k]
+
+        def load_w2(q):
+            if q % QH == 0:
+                stage2[q // QH] = rawp.tile([P, QH, PACK, N], F32, name="raw2", tag="raw")
+            e, g = divmod(q, HG)
+            raw2[q] = stage2[q // QH][:, q % QH]
+            nc.sync.dma_start(
+                out=raw2[q], in_=w2[e, g * KP : (g + 1) * KP, :].rearrange("(p j) n -> p j n", j=PACK)
+            )
+
+        pos1_t = keep.tile([P, T // 16], U16, name="pos1_t")
+        pos2_t = keep.tile([P, T // 16], U16, name="pos2_t")
+        nc.sync.dma_start(pos1_t[:], pos1)
+        nc.sync.dma_start(pos2_t[:], pos2)
+        for es in LOADS1[:-1]:
+            load_w1(es)
+        for q in range(FILL):
+            load_w2(q)
+        load_w1(LOADS1[-1])
+        for q in range(FILL, NQ):
+            load_w2(q)
+        gate_t = rawp.tile([P, 2 * NB, T], F32, name="gate_t", tag="raw")
+        gate_v = gate.flatten_outer_dims().rearrange("(q p) t -> p q t", p=P)
+        for u in (0, NB, 1, NB + 1):
+            nc.sync.dma_start(out=gate_t[:, u, :], in_=gate_v[:, u, :])
+
+        warm = keep.tile([P, 2], F32, name="warm")
+        nc.vector.memset(warm[:, 0:1], 0.0)
+        nc.scalar.activation(out=warm[:, 1:2], in_=warm[:, 0:1], func=GELU)
+
+        xcodes = keep.tile([P, T], U32, name="xcodes", align_bytes=64)
+        xscales = keep.tile([P, T], U8, name="xscales", align_bytes=64)
+        nc.gpsimd.memset(xscales[:], 0)
+        xg = grpp.tile([P, T * PACK], BF16, name="xg", tag="grp1", bufs=6, align_bytes=64)
+        spread_plain(nc, xg[:], xraw[:], 0, T // PACK, False)
+        nc.vector.quantize_mx(out=xcodes[:].bitcast(FP8X4), scales=xscales[:], in_=xg[:])
+        xgc = keep.tile([P, E * C], U32, name="xgc", align_bytes=64)
+        xgs = keep.tile([P, E * C], U8, name="xgs", align_bytes=64)
+
+        def gather_slots(s):
+            sl = slice(s * GSL, (s + 1) * GSL)
+            ol = slice(s * GSL // 16, (s + 1) * GSL // 16)
+            nc.vector.tensor_copy(out=xgc[:, sl], in_=xcodes[:].indirect(offs_t[:, ol]))
+            nc.vector.tensor_copy(out=xgs[:, sl], in_=xscales[:].indirect(offs_t[:, ol]))
+
+        for s in range(E * C // GSL):
+            gather_slots(s)
+
+        ywin = [keep.tile([P, E * C], F32, name="ywin%d" % nb) for nb in range(NB)]
+
+        def copy_w1(e):
+            for g in range(HG):
+                grp1[e, g] = grpp.tile([P, KP * PACK], BF16, name="grp1", tag="grp1", bufs=6, align_bytes=64)
+            mv = 0 if e < 2 else M_VEC
+            spread_w1(nc, grp1[e, 0], raw1[e], 0, 0, P, False)
+            spread_w1(nc, grp1[e, 1], raw1[e], 1, mv, P, True)
+            if mv:
+                spread_w1(nc, grp1[e, 1], raw1[e], 1, 0, mv, False)
+
+        def quant_w1(e):
+            for g in range(HG):
+                c1[e, g] = codep.tile([P, KP], U32, name="c1", tag="c1", align_bytes=64)
+                s1[e, g] = codep.tile([P, KP], U8, name="s1", tag="s1", align_bytes=64)
+                nc.vector.quantize_mx(out=c1[e, g][:].bitcast(FP8X4), scales=s1[e, g][:], in_=grp1[e, g][:])
+
+        def mm1(e):
+            slots = slice(e * C, (e + 1) * C)
+            for g in range(HG):
+                ps1[e, g] = psum.tile([P, PACK, C], F32, name="ps1", tag="ps1", bufs=4)
+                for t in range(PACK):
+                    cols = slice(t * P, (t + 1) * P)
+                    nc.tensor.matmul_mx(
+                        out=ps1[e, g][:, t, :],
+                        lhsT=c1[e, g][:, cols].bitcast(FP8X4),
+                        lhsT_scale=s1[e, g][:, cols],
+                        rhs=xgc[:, slots].bitcast(FP8X4),
+                        rhs_scale=xgs[:, slots],
+                        start=True,
+                        stop=True,
+                    )
+
+        def gelu(e):
+            if e % 2 == 0:
+                hg[e // 2] = grpp.tile([P, 2 * HG * C * PACK], BF16, name="hg", tag="hg", bufs=2, align_bytes=64)
+            for g in range(HG):
+                u = (e % 2) * HG + g
+                nc.scalar.activation(
+                    out=hg[e // 2][:, u * C * PACK : (u + 1) * C * PACK].rearrange("p (n t) -> p n t", t=PACK),
+                    in_=ps1[e, g][:].rearrange("p t n -> p n t"),
+                    func=GELU,
+                )
+
+        def quant_h(pair):
+            hc[pair] = keep.tile([P, 2 * HG * C], U32, name="hc%d" % pair, align_bytes=64)
+            hs[pair] = keep.tile([P, 2 * HG * C], U8, name="hs%d" % pair, align_bytes=64)
+            nc.vector.quantize_mx(out=hc[pair][:].bitcast(FP8X4), scales=hs[pair][:], in_=hg[pair][:])
+
+        def prep_w2(q):
+            grp = grpp.tile([P, N * PACK], BF16, name="grp2", tag="grp2", align_bytes=64)
+            if q == NQ - 1:
+                spread_plain(nc, grp[:], raw2[q], 0, C_VEC_LAST, False)
+                spread_plain(nc, grp[:], raw2[q], C_VEC_LAST, N // PACK, True)
+            else:
+                spread_plain(nc, grp[:], raw2[q], 0, N // PACK, q % 2 == 0)
+            c2[q] = codep.tile([P, N], U32, name="c2", tag="c2", align_bytes=64)
+            s2[q] = codep.tile([P, N], U8, name="s2", tag="s2", align_bytes=64)
+            nc.vector.quantize_mx(out=c2[q][:].bitcast(FP8X4), scales=s2[q][:], in_=grp[:])
+
+        def mm2(q):
+            e, g = divmod(q, HG)
+            u = (e % 2) * HG + g
+            for nb in range(NB):
+                if g == 0:
+                    ps2[e, nb] = psum.tile([P, C], F32, name="ps2_%d" % nb, tag="ps2_%d" % nb, bufs=2)
+                nc.tensor.matmul_mx(
+                    out=ps2[e, nb][:],
+                    lhsT=c2[q][:, nb * P : (nb + 1) * P].bitcast(FP8X4),
+                    lhsT_scale=s2[q][:, nb * P : (nb + 1) * P],
+                    rhs=hc[e // 2][:, u * C : (u + 1) * C].bitcast(FP8X4),
+                    rhs_scale=hs[e // 2][:, u * C : (u + 1) * C],
+                    start=(g == 0),
+                    stop=(g == HG - 1),
+                )
+
+        def y_out(e):
+            for nb in range(NB):
+                copy_on(nc, nb == 1 or e < E - 1, ywin[nb][:, e * C : (e + 1) * C], ps2[e, nb][:])
+
+        for es in LOADS1:
+            for e in es:
+                copy_w1(e)
+                quant_w1(e)
+            for e in es:
+                mm1(e)
+                gelu(e)
+                if e % 2 == 1:
+                    quant_h(e // 2)
+
+        for q in range(NQ):
+            prep_w2(q)
+            mm2(q)
+            if q >= 2 and q % HG == 0:
+                y_out(q // HG - 1)
+        y_out(E - 1)
+
+        prod = {}
+
+        def fetch(nb, r, pos_t):
+            prod[nb, r] = finp.tile([P, T], F32, name="prod%d" % r, tag="prod%d" % r)
+            nc.vector.tensor_tensor(
+                out=prod[nb, r][:], in0=ywin[nb][:].indirect(pos_t[:]), in1=gate_t[:, r * NB + nb, :], op=MULT
+            )
+
+        def add_store(nb, t0, t1):
+            o = finp.tile([P, t1 - t0], F32, name="o", tag="o", bufs=3)
+            nc.vector.tensor_tensor(out=o[:], in0=prod[nb, 0][:, t0:t1], in1=prod[nb, 1][:, t0:t1], op=ADD)
+            nc.sync.dma_start(out=out[nb * P : (nb + 1) * P, t0:t1], in_=o[:])
+
+        fetch(0, 0, pos1_t)
+        fetch(0, 1, pos2_t)
+        fetch(1, 0, pos1_t)
+        add_store(0, 0, T)
+        fetch(1, 1, pos2_t)
+        add_store(1, 0, T // 2)
+        add_store(1, T // 2, T)

@@ -52,7 +52,7 @@ def tile_routed_moe_kernel(tc, xT, w1, w2, gate, offs, pos1, pos2, out):
     nc = tc.nc
     with ExitStack() as ctx:
         keep = ctx.enter_context(tc.tile_pool(name="keep", bufs=1))
-        rawp = ctx.enter_context(tc.tile_pool(name="rawp", bufs=3))
+        rawp = ctx.enter_context(tc.tile_pool(name="rawp", bufs=4))
         grpp = ctx.enter_context(tc.tile_pool(name="grpp", bufs=4))
         codep = ctx.enter_context(tc.tile_pool(name="codep", bufs=6))
         finp = ctx.enter_context(tc.tile_pool(name="finp", bufs=2))

@@ -23,7 +23,6 @@ NB = N // P
 GSL = 256
 NQ = E * HG
 M_VEC = 16
-C_VEC_LAST = 42
 LOADS1 = ((0,), (1,), (2, 3), (4, 5), (6,), (7,))
 FILL = 2
 QH = NQ // 2
@@ -183,14 +182,21 @@ def tile_routed_moe_kernel(tc, xT, w1, w2, gate, offs, pos1, pos2, out):
 
         def prep_w2(q):
             grp = grpp.tile([P, N * PACK], BF16, name="grp2", tag="grp2", align_bytes=64)
-            if q == NQ - 1:
-                spread_plain(nc, grp[:], raw2[q], 0, C_VEC_LAST, False)
-                spread_plain(nc, grp[:], raw2[q], C_VEC_LAST, N // PACK, True)
-            else:
-                spread_plain(nc, grp[:], raw2[q], 0, N // PACK, q % 2 == 0)
             c2[q] = codep.tile([P, N], U32, name="c2", tag="c2", align_bytes=64)
             s2[q] = codep.tile([P, N], U8, name="s2", tag="s2", align_bytes=64)
-            nc.vector.quantize_mx(out=c2[q][:].bitcast(FP8X4), scales=s2[q][:], in_=grp[:])
+            if q == NQ - 1:
+                half = N // PACK // NB
+                spread_plain(nc, grp[:], raw2[q], 0, half, False)
+                spread_plain(nc, grp[:], raw2[q], half, N // PACK, True)
+                for nb in range(NB):
+                    nc.vector.quantize_mx(
+                        out=c2[q][:, nb * P : (nb + 1) * P].bitcast(FP8X4),
+                        scales=s2[q][:, nb * P : (nb + 1) * P],
+                        in_=grp[:, nb * P * PACK : (nb + 1) * P * PACK],
+                    )
+            else:
+                spread_plain(nc, grp[:], raw2[q], 0, N // PACK, q % 2 == 0)
+                nc.vector.quantize_mx(out=c2[q][:].bitcast(FP8X4), scales=s2[q][:], in_=grp[:])
 
         def mm2(q):
             e, g = divmod(q, HG)
@@ -210,7 +216,7 @@ def tile_routed_moe_kernel(tc, xT, w1, w2, gate, offs, pos1, pos2, out):
 
         def y_out(e):
             for nb in range(NB):
-                copy_on(nc, nb == 1 or e < E - 1, ywin[nb][:, e * C : (e + 1) * C], ps2[e, nb][:])
+                copy_on(nc, True, ywin[nb][:, e * C : (e + 1) * C], ps2[e, nb][:])
 
         for es in LOADS1:
             for e in es:
@@ -238,14 +244,15 @@ def tile_routed_moe_kernel(tc, xT, w1, w2, gate, offs, pos1, pos2, out):
             )
 
         def add_store(nb, t0, t1):
-            o = finp.tile([P, t1 - t0], F32, name="o", tag="o", bufs=3)
+            o = finp.tile([P, t1 - t0], F32, name="o", tag="o", bufs=4)
             nc.vector.tensor_tensor(out=o[:], in0=prod[nb, 0][:, t0:t1], in1=prod[nb, 1][:, t0:t1], op=ADD)
             nc.sync.dma_start(out=out[nb * P : (nb + 1) * P, t0:t1], in_=o[:])
 
         fetch(0, 0, pos1_t)
         fetch(0, 1, pos2_t)
         fetch(1, 0, pos1_t)
-        add_store(0, 0, T)
+        add_store(0, 0, T // 2)
         fetch(1, 1, pos2_t)
+        add_store(0, T // 2, T)
         add_store(1, 0, T // 2)
         add_store(1, T // 2, T)

@@ -23,6 +23,7 @@ NB = N // P
 GSL = 256
 NQ = E * HG
 M_VEC = 16
+C_VEC_PREV = 42
 LOADS1 = ((0,), (1,), (2, 3), (4, 5), (6,), (7,))
 FILL = 2
 QH = NQ // 2
@@ -194,6 +195,10 @@ def tile_routed_moe_kernel(tc, xT, w1, w2, gate, offs, pos1, pos2, out):
                         scales=s2[q][:, nb * P : (nb + 1) * P],
                         in_=grp[:, nb * P * PACK : (nb + 1) * P * PACK],
                     )
+            elif q == NQ - 2:
+                spread_plain(nc, grp[:], raw2[q], 0, C_VEC_PREV, False)
+                spread_plain(nc, grp[:], raw2[q], C_VEC_PREV, N // PACK, True)
+                nc.vector.quantize_mx(out=c2[q][:].bitcast(FP8X4), scales=s2[q][:], in_=grp[:])
             else:
                 spread_plain(nc, grp[:], raw2[q], 0, N // PACK, q % 2 == 0)
                 nc.vector.quantize_mx(out=c2[q][:].bitcast(FP8X4), scales=s2[q][:], in_=grp[:])

@@ -1,6 +1,7 @@
 from contextlib import ExitStack
 
 import concourse.mybir as mybir
+from concourse.masks import make_identity
 
 K, T, E, C, H, N = 512, 512, 8, 128, 1024, 256
 FLOPS = 2 * E * C * (K * H + H * N)
@@ -109,6 +110,9 @@ def tile_routed_moe_kernel(tc, xT, w1, w2, gate, offs, pos1, pos2, out):
         gate_v = gate.flatten_outer_dims().rearrange("(q p) t -> p q t", p=P)
         for u in (0, NB, 1, NB + 1):
             nc.sync.dma_start(out=gate_t[:, u, :], in_=gate_v[:, u, :])
+
+        ident = keep.tile([P, P], F32, name="ident")
+        make_identity(nc, ident[:])
 
         warm = keep.tile([P, 2], F32, name="warm")
         nc.vector.memset(warm[:, 0:1], 0.0)
@@ -253,10 +257,15 @@ def tile_routed_moe_kernel(tc, xT, w1, w2, gate, offs, pos1, pos2, out):
             nc.vector.tensor_tensor(out=o[:], in0=prod[nb, 0][:, t0:t1], in1=prod[nb, 1][:, t0:t1], op=ADD)
             nc.sync.dma_start(out=out[nb * P : (nb + 1) * P, t0:t1], in_=o[:])
 
+        acc = psum.tile([P, T // 2], F32, name="acc", tag="ps1", bufs=4)
         fetch(0, 0, pos1_t)
+        nc.tensor.matmul(out=acc[:], lhsT=ident[:], rhs=prod[0, 0][:, 0 : T // 2], start=True, stop=False)
         fetch(0, 1, pos2_t)
+        nc.tensor.matmul(out=acc[:], lhsT=ident[:], rhs=prod[0, 1][:, 0 : T // 2], start=False, stop=True)
+        o0 = finp.tile([P, T // 2], F32, name="o0")
+        nc.scalar.copy(out=o0[:], in_=acc[:])
+        nc.sync.dma_start(out=out[0:P, 0 : T // 2], in_=o0[:])
         fetch(1, 0, pos1_t)
-        add_store(0, 0, T // 2)
         fetch(1, 1, pos2_t)
         add_store(0, T // 2, T)
         add_store(1, 0, T // 2)

@@ -26,7 +26,7 @@ NQ = E * HG
 M_VEC = 16
 C_VEC_PREV = 42
 LOADS1 = ((0,), (1,), (2, 3), (4, 5), (6,), (7,))
-FILL = 2
+CUTS2 = tuple(range(NQ + 1))
 QH = NQ // 2
 
 
@@ -61,7 +61,7 @@ def tile_routed_moe_kernel(tc, xT, w1, w2, gate, offs, pos1, pos2, out):
 
         offs_t = keep.tile([P, E * C // 16], U16, name="offs_t")
         nc.sync.dma_start(offs_t[:], offs)
-        xraw = rawp.tile([P, PACK, T], F32, name="xraw", tag="raw")
+        xraw = rawp.tile([P, PACK, T], F32, name="xraw", tag="one")
         nc.sync.dma_start(out=xraw[:], in_=xT.rearrange("(p j) t -> p j t", j=PACK))
 
         raw1 = {}
@@ -79,21 +79,26 @@ def tile_routed_moe_kernel(tc, xT, w1, w2, gate, offs, pos1, pos2, out):
         hs = {}
 
         def load_w1(es):
-            t1 = rawp.tile([P, len(es), PACK, H], F32, name="raw1", tag="raw")
+            tag, bufs = ("two", 2) if len(es) == 2 else ("one", 4)
+            t1 = rawp.tile([P, len(es), PACK, H], F32, name="raw1", tag=tag, bufs=bufs)
             nc.sync.dma_start(
                 out=t1[:], in_=w1[es[0] : es[0] + len(es)].rearrange("e (p j) h -> p e j h", j=PACK)
             )
             for k, e in enumerate(es):
                 raw1[e] = t1[:, k]
 
-        def load_w2(q):
-            if q % QH == 0:
-                stage2[q // QH] = rawp.tile([P, QH, PACK, N], F32, name="raw2", tag="raw")
-            e, g = divmod(q, HG)
-            raw2[q] = stage2[q // QH][:, q % QH]
+        def load_w2(q0, q1):
+            if q0 in (0, QH // 2):
+                stage2[0] = rawp.tile([P, QH // 2, PACK, N], F32, name="raw2", tag="one"), q0
+            elif q0 == QH:
+                stage2[0] = rawp.tile([P, QH, PACK, N], F32, name="raw2", tag="two", bufs=2), q0
+            stage, first = stage2[0]
             nc.sync.dma_start(
-                out=raw2[q], in_=w2[e, g * KP : (g + 1) * KP, :].rearrange("(p j) n -> p j n", j=PACK)
+                out=stage[:, q0 - first : q1 - first],
+                in_=w2.flatten_outer_dims()[q0 * KP : q1 * KP, :].rearrange("(q p j) n -> p q j n", p=P, j=PACK),
             )
+            for q in range(q0, q1):
+                raw2[q] = stage[:, q - first]
 
         pos1_t = keep.tile([P, T // 16], U16, name="pos1_t")
         pos2_t = keep.tile([P, T // 16], U16, name="pos2_t")
@@ -101,12 +106,10 @@ def tile_routed_moe_kernel(tc, xT, w1, w2, gate, offs, pos1, pos2, out):
         nc.sync.dma_start(pos2_t[:], pos2)
         for es in LOADS1[:-1]:
             load_w1(es)
-        for q in range(FILL):
-            load_w2(q)
         load_w1(LOADS1[-1])
-        for q in range(FILL, NQ):
-            load_w2(q)
-        gate_t = rawp.tile([P, 2 * NB, T], F32, name="gate_t", tag="raw")
+        for q0, q1 in zip(CUTS2, CUTS2[1:]):
+            load_w2(q0, q1)
+        gate_t = rawp.tile([P, 2 * NB, T], F32, name="gate_t", tag="one")
         gate_v = gate.flatten_outer_dims().rearrange("(q p) t -> p q t", p=P)
         for u in (0, NB, 1, NB + 1):
             nc.sync.dma_start(out=gate_t[:, u, :], in_=gate_v[:, u, :])

@@ -23,7 +23,7 @@ HG = H // KP
 NB = N // P
 GSL = 256
 NQ = E * HG
-M_VEC = 16
+M_VEC = 48
 C_VEC_PREV = 42
 LOADS1 = ((0,), (1,), (2, 3), (4, 5), (6,), (7,))
 CUTS2 = tuple(range(NQ + 1))

@@ -24,7 +24,6 @@ NB = N // P
 GSL = 256
 NQ = E * HG
 M_VEC = 48
-C_VEC_PREV = 42
 LOADS1 = ((0,), (1,), (2, 3), (4, 5), (6,), (7,))
 CUTS2 = tuple(range(NQ + 1))
 QH = NQ // 2
@@ -93,10 +92,12 @@ def tile_routed_moe_kernel(tc, xT, w1, w2, gate, offs, pos1, pos2, out):
             elif q0 == QH:
                 stage2[0] = rawp.tile([P, QH, PACK, N], F32, name="raw2", tag="two", bufs=2), q0
             stage, first = stage2[0]
-            nc.sync.dma_start(
-                out=stage[:, q0 - first : q1 - first],
-                in_=w2.flatten_outer_dims()[q0 * KP : q1 * KP, :].rearrange("(q p j) n -> p q j n", p=P, j=PACK),
-            )
+            src = w2.flatten_outer_dims()[q0 * KP : q1 * KP, :].rearrange("(q p j) n -> p q j n", p=P, j=PACK)
+            width = P if q1 == NQ else N
+            for n0 in range(0, N, width):
+                nc.sync.dma_start(
+                    out=stage[:, q0 - first : q1 - first, :, n0 : n0 + width], in_=src[:, :, :, n0 : n0 + width]
+                )
             for q in range(q0, q1):
                 raw2[q] = stage[:, q - first]
 
@@ -190,36 +191,40 @@ def tile_routed_moe_kernel(tc, xT, w1, w2, gate, offs, pos1, pos2, out):
 
         def prep_w2(q):
             grp = grpp.tile([P, N * PACK], BF16, name="grp2", tag="grp2", align_bytes=64)
-            c2[q] = codep.tile([P, N], U32, name="c2", tag="c2", align_bytes=64)
-            s2[q] = codep.tile([P, N], U8, name="s2", tag="s2", align_bytes=64)
-            if q == NQ - 1:
-                half = N // PACK // NB
-                spread_plain(nc, grp[:], raw2[q], 0, half, False)
-                spread_plain(nc, grp[:], raw2[q], half, N // PACK, True)
-                for nb in range(NB):
-                    nc.vector.quantize_mx(
-                        out=c2[q][:, nb * P : (nb + 1) * P].bitcast(FP8X4),
-                        scales=s2[q][:, nb * P : (nb + 1) * P],
-                        in_=grp[:, nb * P * PACK : (nb + 1) * P * PACK],
-                    )
-            elif q == NQ - 2:
-                spread_plain(nc, grp[:], raw2[q], 0, C_VEC_PREV, False)
-                spread_plain(nc, grp[:], raw2[q], C_VEC_PREV, N // PACK, True)
-                nc.vector.quantize_mx(out=c2[q][:].bitcast(FP8X4), scales=s2[q][:], in_=grp[:])
-            else:
-                spread_plain(nc, grp[:], raw2[q], 0, N // PACK, q % 2 == 0)
-                nc.vector.quantize_mx(out=c2[q][:].bitcast(FP8X4), scales=s2[q][:], in_=grp[:])
+            codes = codep.tile([P, N], U32, name="c2", tag="c2", align_bytes=64)
+            scales = codep.tile([P, N], U8, name="s2", tag="s2", align_bytes=64)
+            spread_plain(nc, grp[:], raw2[q], 0, N // PACK, q % 2 == 0)
+            nc.vector.quantize_mx(out=codes[:].bitcast(FP8X4), scales=scales[:], in_=grp[:])
+            for nb in range(NB):
+                c2[q, nb] = codes[:, nb * P : (nb + 1) * P]
+                s2[q, nb] = scales[:, nb * P : (nb + 1) * P]
 
-        def mm2(q):
+        def prep_last(nb):
+            grp = grpp.tile([P, HG * P * PACK], BF16, name="grp2", tag="grp2", align_bytes=64)
+            codes = codep.tile([P, HG * P], U32, name="c2", tag="c2", align_bytes=64)
+            scales = codep.tile([P, HG * P], U8, name="s2", tag="s2", align_bytes=64)
+            for g in range(HG):
+                q = NQ - HG + g
+                part = slice(g * P * PACK, (g + 1) * P * PACK)
+                cols = slice(g * P, (g + 1) * P)
+                spread_plain(nc, grp[:, part], raw2[q][:, :, nb * P : (nb + 1) * P], 0, P // PACK, nb == 1)
+                if nb == 0:
+                    nc.vector.quantize_mx(out=codes[:, cols].bitcast(FP8X4), scales=scales[:, cols], in_=grp[:, part])
+                c2[q, nb] = codes[:, cols]
+                s2[q, nb] = scales[:, cols]
+            if nb == 1:
+                nc.vector.quantize_mx(out=codes[:].bitcast(FP8X4), scales=scales[:], in_=grp[:])
+
+        def mm2(q, blocks=tuple(range(NB))):
             e, g = divmod(q, HG)
             u = (e % 2) * HG + g
-            for nb in range(NB):
+            for nb in blocks:
                 if g == 0:
                     ps2[e, nb] = psum.tile([P, C], F32, name="ps2_%d" % nb, tag="ps2_%d" % nb, bufs=2)
                 nc.tensor.matmul_mx(
                     out=ps2[e, nb][:],
-                    lhsT=c2[q][:, nb * P : (nb + 1) * P].bitcast(FP8X4),
-                    lhsT_scale=s2[q][:, nb * P : (nb + 1) * P],
+                    lhsT=c2[q, nb].bitcast(FP8X4),
+                    lhsT_scale=s2[q, nb],
                     rhs=hc[e // 2][:, u * C : (u + 1) * C].bitcast(FP8X4),
                     rhs_scale=hs[e // 2][:, u * C : (u + 1) * C],
                     start=(g == 0),
@@ -240,11 +245,16 @@ def tile_routed_moe_kernel(tc, xT, w1, w2, gate, offs, pos1, pos2, out):
                 if e % 2 == 1:
                     quant_h(e // 2)
 
-        for q in range(NQ):
+        for q in range(NQ - HG):
             prep_w2(q)
             mm2(q)
             if q >= 2 and q % HG == 0:
                 y_out(q // HG - 1)
+        y_out(E - 2)
+        for nb in range(NB):
+            prep_last(nb)
+            for q in range(NQ - HG, NQ):
+                mm2(q, (nb,))
         y_out(E - 1)
 
         prod = {}

@@ -59,9 +59,9 @@ def tile_routed_moe_kernel(tc, xT, w1, w2, gate, offs, pos1, pos2, out):
         psum = ctx.enter_context(tc.psum_pool(name="psum", bufs=2))
 
         offs_t = keep.tile([P, E * C // 16], U16, name="offs_t")
-        nc.sync.dma_start(offs_t[:], offs)
         xraw = rawp.tile([P, PACK, T], F32, name="xraw", tag="one")
         nc.sync.dma_start(out=xraw[:], in_=xT.rearrange("(p j) t -> p j t", j=PACK))
+        nc.sync.dma_start(offs_t[:], offs)
 
         raw1 = {}
         raw2 = {}

@@ -207,9 +207,19 @@ def tile_routed_moe_kernel(tc, xT, w1, w2, gate, offs, pos1, pos2, out):
                 q = NQ - HG + g
                 part = slice(g * P * PACK, (g + 1) * P * PACK)
                 cols = slice(g * P, (g + 1) * P)
-                spread_plain(nc, grp[:, part], raw2[q][:, :, nb * P : (nb + 1) * P], 0, P // PACK, nb == 1)
-                if nb == 0:
-                    nc.vector.quantize_mx(out=codes[:, cols].bitcast(FP8X4), scales=scales[:, cols], in_=grp[:, part])
+                cuts = 2 if (nb, g) == (0, HG - 1) else 1
+                wide = P // cuts
+                for i in range(cuts):
+                    groups = wide // PACK
+                    block = raw2[q][:, :, nb * P : (nb + 1) * P]
+                    spread_plain(nc, grp[:, part], block, i * groups, (i + 1) * groups, nb == 1)
+                for i in range(cuts if nb == 0 else 0):
+                    c0 = g * P + i * wide
+                    nc.vector.quantize_mx(
+                        out=codes[:, c0 : c0 + wide].bitcast(FP8X4),
+                        scales=scales[:, c0 : c0 + wide],
+                        in_=grp[:, c0 * PACK : (c0 + wide) * PACK],
+                    )
                 c2[q, nb] = codes[:, cols]
                 s2[q, nb] = scales[:, cols]
             if nb == 1:

from contextlib import ExitStack

import concourse.mybir as mybir
from concourse.masks import make_identity

K, T, E, C, H, N = 512, 512, 8, 128, 1024, 256
FLOPS = 2 * E * C * (K * H + H * N)

F32 = mybir.dt.float32
BF16 = mybir.dt.bfloat16
U32 = mybir.dt.uint32
U16 = mybir.dt.uint16
U8 = mybir.dt.uint8
FP8X4 = mybir.dt.float8_e4m3fn_x4
GELU = mybir.ActivationFunctionType.Gelu_apprx_tanh
MULT = mybir.AluOpType.mult
ADD = mybir.AluOpType.add

P = 128
PACK = 4
KP = P * PACK
HG = H // KP
NB = N // P
GSL = 256
NQ = E * HG
M_VEC = 48
LOADS1 = ((0,), (1,), (2, 3), (4, 5), (6,), (7,))
CUTS2 = tuple(range(NQ + 1))
QH = NQ // 2


def copy_on(nc, scalar, dst, src):
    if scalar:
        nc.scalar.copy(out=dst, in_=src)
    else:
        nc.vector.tensor_copy(out=dst, in_=src)


def spread_w1(nc, grp, raw, g, m0, m1, scalar):
    src = raw[:, :, g * KP : (g + 1) * KP].rearrange("p j (m t) -> p m j t", t=PACK)
    dst = grp.rearrange("p (t m j) -> p m j t", t=PACK, j=PACK)
    copy_on(nc, scalar, dst[:, m0:m1], src[:, m0:m1])


def spread_plain(nc, grp, raw, c0, c1, scalar):
    src = raw.rearrange("p j (c i) -> p c j i", i=PACK)
    dst = grp.rearrange("p (c i j) -> p c j i", i=PACK, j=PACK)
    copy_on(nc, scalar, dst[:, c0:c1], src[:, c0:c1])


def tile_routed_moe_kernel(tc, xT, w1, w2, gate, offs, pos1, pos2, out):
    nc = tc.nc
    with ExitStack() as ctx:
        keep = ctx.enter_context(tc.tile_pool(name="keep", bufs=1))
        rawp = ctx.enter_context(tc.tile_pool(name="rawp", bufs=4))
        grpp = ctx.enter_context(tc.tile_pool(name="grpp", bufs=4))
        codep = ctx.enter_context(tc.tile_pool(name="codep", bufs=6))
        finp = ctx.enter_context(tc.tile_pool(name="finp", bufs=2))
        psum = ctx.enter_context(tc.psum_pool(name="psum", bufs=2))

        offs_t = keep.tile([P, E * C // 16], U16, name="offs_t")
        xraw = rawp.tile([P, PACK, T], F32, name="xraw", tag="one")
        nc.sync.dma_start(out=xraw[:], in_=xT.rearrange("(p j) t -> p j t", j=PACK))
        nc.sync.dma_start(offs_t[:], offs)

        raw1 = {}
        raw2 = {}
        stage2 = {}
        grp1 = {}
        c1 = {}
        s1 = {}
        c2 = {}
        s2 = {}
        ps1 = {}
        ps2 = {}
        hg = {}
        hc = {}
        hs = {}

        def load_w1(es):
            tag, bufs = ("two", 2) if len(es) == 2 else ("one", 4)
            t1 = rawp.tile([P, len(es), PACK, H], F32, name="raw1", tag=tag, bufs=bufs)
            nc.sync.dma_start(
                out=t1[:], in_=w1[es[0] : es[0] + len(es)].rearrange("e (p j) h -> p e j h", j=PACK)
            )
            for k, e in enumerate(es):
                raw1[e] = t1[:, k]

        def load_w2(q0, q1):
            if q0 in (0, QH // 2):
                stage2[0] = rawp.tile([P, QH // 2, PACK, N], F32, name="raw2", tag="one"), q0
            elif q0 == QH:
                stage2[0] = rawp.tile([P, QH, PACK, N], F32, name="raw2", tag="two", bufs=2), q0
            stage, first = stage2[0]
            src = w2.flatten_outer_dims()[q0 * KP : q1 * KP, :].rearrange("(q p j) n -> p q j n", p=P, j=PACK)
            width = P if q1 == NQ else N
            for n0 in range(0, N, width):
                nc.sync.dma_start(
                    out=stage[:, q0 - first : q1 - first, :, n0 : n0 + width], in_=src[:, :, :, n0 : n0 + width]
                )
            for q in range(q0, q1):
                raw2[q] = stage[:, q - first]

        pos1_t = keep.tile([P, T // 16], U16, name="pos1_t")
        pos2_t = keep.tile([P, T // 16], U16, name="pos2_t")
        nc.sync.dma_start(pos1_t[:], pos1)
        nc.sync.dma_start(pos2_t[:], pos2)
        for es in LOADS1[:-1]:
            load_w1(es)
        load_w1(LOADS1[-1])
        for q0, q1 in zip(CUTS2, CUTS2[1:]):
            load_w2(q0, q1)
        gate_t = rawp.tile([P, 2 * NB, T], F32, name="gate_t", tag="one")
        gate_v = gate.flatten_outer_dims().rearrange("(q p) t -> p q t", p=P)
        for u in (0, NB, 1, NB + 1):
            nc.sync.dma_start(out=gate_t[:, u, :], in_=gate_v[:, u, :])

        ident = keep.tile([P, P], F32, name="ident")
        make_identity(nc, ident[:])

        warm = keep.tile([P, 2], F32, name="warm")
        nc.vector.memset(warm[:, 0:1], 0.0)
        nc.scalar.activation(out=warm[:, 1:2], in_=warm[:, 0:1], func=GELU)

        xcodes = keep.tile([P, T], U32, name="xcodes", align_bytes=64)
        xscales = keep.tile([P, T], U8, name="xscales", align_bytes=64)
        nc.gpsimd.memset(xscales[:], 0)
        xg = grpp.tile([P, T * PACK], BF16, name="xg", tag="grp1", bufs=6, align_bytes=64)
        spread_plain(nc, xg[:], xraw[:], 0, T // PACK, False)
        nc.vector.quantize_mx(out=xcodes[:].bitcast(FP8X4), scales=xscales[:], in_=xg[:])
        xgc = keep.tile([P, E * C], U32, name="xgc", align_bytes=64)
        xgs = keep.tile([P, E * C], U8, name="xgs", align_bytes=64)

        def gather_slots(s):
            sl = slice(s * GSL, (s + 1) * GSL)
            ol = slice(s * GSL // 16, (s + 1) * GSL // 16)
            nc.vector.tensor_copy(out=xgc[:, sl], in_=xcodes[:].indirect(offs_t[:, ol]))
            nc.vector.tensor_copy(out=xgs[:, sl], in_=xscales[:].indirect(offs_t[:, ol]))

        for s in range(E * C // GSL):
            gather_slots(s)

        ywin = [keep.tile([P, E * C], F32, name="ywin%d" % nb) for nb in range(NB)]

        def copy_w1(e):
            for g in range(HG):
                grp1[e, g] = grpp.tile([P, KP * PACK], BF16, name="grp1", tag="grp1", bufs=6, align_bytes=64)
            mv = 0 if e < 2 else M_VEC
            spread_w1(nc, grp1[e, 0], raw1[e], 0, 0, P, False)
            spread_w1(nc, grp1[e, 1], raw1[e], 1, mv, P, True)
            if mv:
                spread_w1(nc, grp1[e, 1], raw1[e], 1, 0, mv, False)

        def quant_w1(e):
            for g in range(HG):
                c1[e, g] = codep.tile([P, KP], U32, name="c1", tag="c1", align_bytes=64)
                s1[e, g] = codep.tile([P, KP], U8, name="s1", tag="s1", align_bytes=64)
                nc.vector.quantize_mx(out=c1[e, g][:].bitcast(FP8X4), scales=s1[e, g][:], in_=grp1[e, g][:])

        def mm1(e):
            slots = slice(e * C, (e + 1) * C)
            for g in range(HG):
                ps1[e, g] = psum.tile([P, PACK, C], F32, name="ps1", tag="ps1", bufs=4)
                for t in range(PACK):
                    cols = slice(t * P, (t + 1) * P)
                    nc.tensor.matmul_mx(
                        out=ps1[e, g][:, t, :],
                        lhsT=c1[e, g][:, cols].bitcast(FP8X4),
                        lhsT_scale=s1[e, g][:, cols],
                        rhs=xgc[:, slots].bitcast(FP8X4),
                        rhs_scale=xgs[:, slots],
                        start=True,
                        stop=True,
                    )

        def gelu(e):
            if e % 2 == 0:
                hg[e // 2] = grpp.tile([P, 2 * HG * C * PACK], BF16, name="hg", tag="hg", bufs=2, align_bytes=64)
            for g in range(HG):
                u = (e % 2) * HG + g
                nc.scalar.activation(
                    out=hg[e // 2][:, u * C * PACK : (u + 1) * C * PACK].rearrange("p (n t) -> p n t", t=PACK),
                    in_=ps1[e, g][:].rearrange("p t n -> p n t"),
                    func=GELU,
                )

        def quant_h(pair):
            hc[pair] = keep.tile([P, 2 * HG * C], U32, name="hc%d" % pair, align_bytes=64)
            hs[pair] = keep.tile([P, 2 * HG * C], U8, name="hs%d" % pair, align_bytes=64)
            nc.vector.quantize_mx(out=hc[pair][:].bitcast(FP8X4), scales=hs[pair][:], in_=hg[pair][:])

        def prep_w2(q):
            grp = grpp.tile([P, N * PACK], BF16, name="grp2", tag="grp2", align_bytes=64)
            codes = codep.tile([P, N], U32, name="c2", tag="c2", align_bytes=64)
            scales = codep.tile([P, N], U8, name="s2", tag="s2", align_bytes=64)
            spread_plain(nc, grp[:], raw2[q], 0, N // PACK, q % 2 == 0)
            nc.vector.quantize_mx(out=codes[:].bitcast(FP8X4), scales=scales[:], in_=grp[:])
            for nb in range(NB):
                c2[q, nb] = codes[:, nb * P : (nb + 1) * P]
                s2[q, nb] = scales[:, nb * P : (nb + 1) * P]

        def prep_last(nb):
            grp = grpp.tile([P, HG * P * PACK], BF16, name="grp2", tag="grp2", align_bytes=64)
            codes = codep.tile([P, HG * P], U32, name="c2", tag="c2", align_bytes=64)
            scales = codep.tile([P, HG * P], U8, name="s2", tag="s2", align_bytes=64)
            for g in range(HG):
                q = NQ - HG + g
                part = slice(g * P * PACK, (g + 1) * P * PACK)
                cols = slice(g * P, (g + 1) * P)
                cuts = 2 if (nb, g) == (0, HG - 1) else 1
                wide = P // cuts
                for i in range(cuts):
                    groups = wide // PACK
                    block = raw2[q][:, :, nb * P : (nb + 1) * P]
                    spread_plain(nc, grp[:, part], block, i * groups, (i + 1) * groups, nb == 1)
                for i in range(cuts if nb == 0 else 0):
                    c0 = g * P + i * wide
                    nc.vector.quantize_mx(
                        out=codes[:, c0 : c0 + wide].bitcast(FP8X4),
                        scales=scales[:, c0 : c0 + wide],
                        in_=grp[:, c0 * PACK : (c0 + wide) * PACK],
                    )
                c2[q, nb] = codes[:, cols]
                s2[q, nb] = scales[:, cols]
            if nb == 1:
                nc.vector.quantize_mx(out=codes[:].bitcast(FP8X4), scales=scales[:], in_=grp[:])

        def mm2(q, blocks=tuple(range(NB))):
            e, g = divmod(q, HG)
            u = (e % 2) * HG + g
            for nb in blocks:
                if g == 0:
                    ps2[e, nb] = psum.tile([P, C], F32, name="ps2_%d" % nb, tag="ps2_%d" % nb, bufs=2)
                nc.tensor.matmul_mx(
                    out=ps2[e, nb][:],
                    lhsT=c2[q, nb].bitcast(FP8X4),
                    lhsT_scale=s2[q, nb],
                    rhs=hc[e // 2][:, u * C : (u + 1) * C].bitcast(FP8X4),
                    rhs_scale=hs[e // 2][:, u * C : (u + 1) * C],
                    start=(g == 0),
                    stop=(g == HG - 1),
                )

        def y_out(e):
            for nb in range(NB):
                copy_on(nc, True, ywin[nb][:, e * C : (e + 1) * C], ps2[e, nb][:])

        for es in LOADS1:
            for e in es:
                copy_w1(e)
                quant_w1(e)
            for e in es:
                mm1(e)
                gelu(e)
                if e % 2 == 1:
                    quant_h(e // 2)

        for q in range(NQ - HG):
            prep_w2(q)
            mm2(q)
            if q >= 2 and q % HG == 0:
                y_out(q // HG - 1)
        y_out(E - 2)
        for nb in range(NB):
            prep_last(nb)
            for q in range(NQ - HG, NQ):
                mm2(q, (nb,))
        y_out(E - 1)

        prod = {}

        def fetch(nb, r, pos_t):
            prod[nb, r] = finp.tile([P, T], F32, name="prod%d" % r, tag="prod%d" % r)
            nc.vector.tensor_tensor(
                out=prod[nb, r][:], in0=ywin[nb][:].indirect(pos_t[:]), in1=gate_t[:, r * NB + nb, :], op=MULT
            )

        def add_store(nb, t0, t1):
            o = finp.tile([P, t1 - t0], F32, name="o", tag="o", bufs=4)
            nc.vector.tensor_tensor(out=o[:], in0=prod[nb, 0][:, t0:t1], in1=prod[nb, 1][:, t0:t1], op=ADD)
            nc.sync.dma_start(out=out[nb * P : (nb + 1) * P, t0:t1], in_=o[:])

        acc = psum.tile([P, T // 2], F32, name="acc", tag="ps1", bufs=4)
        fetch(0, 0, pos1_t)
        nc.tensor.matmul(out=acc[:], lhsT=ident[:], rhs=prod[0, 0][:, 0 : T // 2], start=True, stop=False)
        fetch(0, 1, pos2_t)
        nc.tensor.matmul(out=acc[:], lhsT=ident[:], rhs=prod[0, 1][:, 0 : T // 2], start=False, stop=True)
        o0 = finp.tile([P, T // 2], F32, name="o0")
        nc.scalar.copy(out=o0[:], in_=acc[:])
        nc.sync.dma_start(out=out[0:P, 0 : T // 2], in_=o0[:])
        fetch(1, 0, pos1_t)
        fetch(1, 1, pos2_t)
        add_store(0, T // 2, T)
        add_store(1, 0, T // 2)
        add_store(1, T // 2, T)
